import numpy as np
import ml_dtypes


def mxq(x, axis, fmt="e4m3"):
    dtype, down = {"e4m3": (ml_dtypes.float8_e4m3fn, 7), "e5m2": (ml_dtypes.float8_e5m2, 14)}[fmt]
    v = np.moveaxis(np.asarray(x, np.float32).astype(ml_dtypes.bfloat16).astype(np.float64), axis, -1)
    blocks = v.reshape(v.shape[:-1] + (-1, 32))
    amax = np.abs(blocks).max(-1, keepdims=True)
    byte = np.maximum(np.where(amax > 0, np.frexp(amax)[1] - 1 + 127, 0) - down, 1)
    scale = np.exp2(byte - 127.0)
    codes = (blocks / scale).astype(np.float32).astype(dtype).astype(np.float64)
    return np.moveaxis((codes * scale).reshape(v.shape), -1, axis)


WIDE = False


def mx_kscale(k):
    if not WIDE:
        return np.ones(k)
    levels = np.array([10, -10, 5, -5, 0])
    if k % 512:
        return np.exp2(np.random.permutation(np.resize(levels, k // 32))).repeat(32)
    a = np.empty((k // 512, 16))
    for p in range(k // 512):
        a[p, :8] = np.random.permutation(np.resize(levels, 8))
        for g in range(8):
            far = levels[np.abs(levels - a[p, g]) >= 10]
            a[p, g + 8] = far[np.random.randint(len(far))]
    return np.exp2(a.ravel()).repeat(32)


BF16 = ml_dtypes.bfloat16


def bf(x):
    return np.asarray(x, np.float32).astype(BF16)


def f64(x):
    return np.asarray(x).astype(np.float64)


D, T, K, N, F = 2, 1024, 512, 1024, 1536


def draw0():
    s = mx_kscale(N)
    t = mx_kscale(T)
    return {
        "x": bf(np.random.standard_normal((D, T, K)) / np.sqrt(T) / t[:, None]),
        "dy": bf(np.random.standard_normal((D, T, N)) * s * t[:, None]),
        "w2": bf(np.random.standard_normal((F, N)) / np.sqrt(N) / s),
        "g": bf(np.random.uniform(0.1, 1.1, (D, T, F))),
        "c": bf(np.random.uniform(0.3, 0.8, (D,))),
    }


def core(x, dy, w2, g, c):
    x, dy, g, c = f64(x), f64(dy), f64(g), f64(c)
    w2q = mxq(f64(w2), 1, "e4m3")
    dw = np.zeros((K, F))
    for d in range(D):
        dh = (mxq(dy[d], 1, "e4m3") @ w2q.T) * g[d]
        part = mxq(x[d], 0, "e4m3").T @ mxq(dh, 0, "e4m3")
        dw = dw + c[d] * part
    return dw


def e4m3fn_bytes(y):
    return np.clip(np.asarray(y, np.float64), -448.0, 448.0).astype(np.float32).astype(ml_dtypes.float8_e4m3fn).view(np.uint8)


def e4m3fn_values(b):
    return np.asarray(b, np.uint8).view(ml_dtypes.float8_e4m3fn).astype(np.float64)


def setup_inputs():
    d = draw0()
    x0 = np.asarray(d['w2']).astype(np.float64)
    s = (np.max(np.abs(x0), axis=(0,), keepdims=True) / 448.0).astype(np.float32)
    out = {}
    for k, v in d.items():
        if k == 'w2':
            out['w2_bytes'] = e4m3fn_bytes(x0 / s.astype(np.float64))
            out['w2_scale'] = s
        else:
            out[k] = v
    return out


def reference(x, dy, w2_bytes, w2_scale, g, c):
    return core(x, dy, e4m3fn_values(w2_bytes) * w2_scale.astype(np.float64), g, c)

@@ -1,0 +1,558 @@
+from contextlib import ExitStack
+
+import concourse.mybir as mybir
+from concourse.masks import make_identity
+
+D, T, K, N, F = 2, 1024, 512, 1024, 1536
+FLOPS = 2 * D * T * N * F + 2 * D * T * K * F
+
+F32 = mybir.dt.float32
+BF16 = mybir.dt.bfloat16
+U32 = mybir.dt.uint32
+U8 = mybir.dt.uint8
+FP8 = mybir.dt.float8_e4m3fn
+FP8X4 = mybir.dt.float8_e4m3fn_x4
+MULT = mybir.AluOpType.mult
+ADD = mybir.AluOpType.add
+COPY = mybir.ActivationFunctionType.Copy
+
+P = 128
+HALVES = 2
+PAIRS = 6
+PF = 256
+SEQ = [(0, j) for j in range(6)] + [(1, j) for j in range(6)]
+
+
+def tile_shard_weight_grad_s7_kernel(tc, x, dy, w2_bytes, w2_scale, g, c, out):
+    nc = tc.nc
+    with ExitStack() as ctx:
+        keep = ctx.enter_context(tc.tile_pool(name="keep", bufs=1))
+        work = ctx.enter_context(tc.tile_pool(name="work", bufs=2))
+        psum = ctx.enter_context(tc.psum_pool(name="psum", bufs=2))
+        ctx.enter_context(tc.manual_schedule())
+
+        scale_col = keep.tile([P, 8], F32, name="scale_col")
+        nc.scalar.dma_start(out=scale_col[:], in_=w2_scale.rearrange("o (p c) -> p (o c)", c=8))
+        c_bf = keep.tile([P, D], BF16, name="c_bf")
+        nc.scalar.dma_start(out=c_bf[:], in_=c.partition_broadcast(P))
+
+        w_raw, y_raw, x_raw, g_raw = {}, {}, {}, {}
+        w_view = w2_bytes.rearrange("(j b p) n -> j p b n", b=2, p=P)
+        out_view = out.rearrange("(h kt p) f -> h p kt f", kt=2, p=P)
+
+        def load_w(j):
+            w_raw[j] = work.tile([P, 2, N], U8, name="w_raw", bufs=PAIRS)
+            nc.sync.dma_start(out=w_raw[j][:], in_=w_view[j])
+
+        def load_y(dd, q, tp):
+            y_raw[dd, q, tp] = work.tile([P, 2, N], BF16, name="y_raw", bufs=8, align_bytes=64)
+            nc.sync.dma_start(
+                out=y_raw[dd, q, tp][:],
+                in_=dy[dd].rearrange("(q p t) n -> q p t n", q=2, t=4)[q][:, 2 * tp : 2 * tp + 2, :],
+            )
+
+        def load_x(dd, q):
+            x_raw[dd, q] = work.tile([P, 4, K], BF16, name="x_raw", bufs=4, align_bytes=64)
+            nc.sync.dma_start(out=x_raw[dd, q][:], in_=x[dd].rearrange("(q p t) k -> q p t k", q=2, t=4)[q])
+
+        def load_g(dd, q, ch):
+            g_raw[dd, q, ch] = work.tile([P, 4, 512], BF16, name="g_raw", bufs=8, align_bytes=64)
+            nc.sync.dma_start(
+                out=g_raw[dd, q, ch][:],
+                in_=g[dd].rearrange("(q p t) f -> q p t f", q=2, t=4)[q][:, :, 512 * ch : 512 * (ch + 1)],
+            )
+
+        load_w(0)
+        load_y(0, 0, 0)
+        load_w(1)
+        load_y(0, 0, 1)
+        load_y(0, 1, 0)
+        load_w(2)
+        load_y(0, 1, 1)
+        load_g(0, 0, 0)
+        load_x(0, 0)
+        load_g(0, 1, 0)
+        load_x(0, 1)
+        load_w(3)
+        load_g(0, 0, 1)
+        load_g(0, 1, 1)
+        load_w(4)
+        load_w(5)
+        for q in range(2):
+            for tp in range(2):
+                load_y(1, q, tp)
+        load_g(0, 0, 2)
+        load_g(0, 1, 2)
+        load_x(1, 0)
+        load_x(1, 1)
+        load_g(1, 0, 0)
+        load_g(1, 1, 0)
+
+        ident = keep.tile([P, P], F32, name="ident", align_bytes=64)
+        make_identity(nc, ident[:])
+        scale_all = keep.tile([P, P, 8], F32, name="scale_all", align_bytes=64)
+        for h in range(2):
+            ps = psum.tile([P, 4, P], F32, name="tr", bufs=2)
+            for cc in range(4):
+                col = 4 * h + cc
+                nc.tensor.transpose(ps[:, cc, :], scale_col[:, col : col + 1].to_broadcast([P, P]), ident[:])
+            view = ps[:].rearrange("p c j -> p j c")
+            if h == 0:
+                nc.scalar.copy(out=scale_all[:, :, 0:4], in_=view)
+            else:
+                nc.vector.tensor_copy(out=scale_all[:, :, 4:8], in_=view)
+        c_all = keep.tile([P, D], F32, name="c_all")
+        nc.scalar.copy(out=c_all[:], in_=c_bf[:])
+
+        wb, gw, w_codes, w_scales = {}, {}, {}, {}
+        gy, y_codes, y_scales = {}, {}, {}
+        x_codes, x_scales, gx = {}, {}, {}
+        bank = {}
+        dh, d_codes, d_scales = {}, {}, {}
+        acc = {}
+
+        def prod(b):
+            wb[b] = work.tile([P, N], BF16, name="wb", bufs=7, align_bytes=64)
+            nc.vector.tensor_tensor(
+                out=wb[b][:],
+                in0=w_raw[b // 2][:, b % 2, :].bitcast(FP8),
+                in1=scale_all[:].rearrange("p j c -> p (j c)"),
+                op=MULT,
+            )
+
+        def word_transposes(words, ps):
+            for gi in range(2):
+                for u in range(2):
+                    nc.tensor.transpose(ps[:, gi, u, :], words[:, 256 * gi + u : 256 * (gi + 1) : 2], ident[:])
+
+        def wtr(b):
+            ps = psum.tile([P, 2, 2, P], F32, name="tr", bufs=2)
+            word_transposes(wb[b][:].bitcast(F32), ps)
+            bank["w", b] = ps
+
+        def wex(b):
+            j = b // 2
+            if j not in gw:
+                gw[j] = work.tile([P, 2, 2, P, 4], BF16, name="gw", bufs=2, align_bytes=64)
+            dst = gw[j][:, b % 2].rearrange("p g f t -> p (g f t)").bitcast(F32)
+            nc.scalar.copy(
+                out=dst.rearrange("p (g f u) -> p g f u", g=2, u=2),
+                in_=bank["w", b][:].rearrange("p g u f -> p g f u"),
+            )
+
+        def wq(j):
+            w_codes[j] = work.tile([P, 2, 2, P], U32, name="w_codes", bufs=PAIRS, align_bytes=64)
+            w_scales[j] = work.tile([P, 2, 2, P], U8, name="w_scales", bufs=PAIRS, align_bytes=64)
+            nc.vector.quantize_mx(
+                out=w_codes[j][:].rearrange("p b g f -> p (b g f)").bitcast(FP8X4),
+                scales=w_scales[j][:].rearrange("p b g f -> p (b g f)"),
+                in_=gw[j][:].rearrange("p b g f t -> p (b g f t)"),
+            )
+
+        def ytr(dd, q, t):
+            ps = psum.tile([P, 2, 2, P], F32, name="tr", bufs=2)
+            word_transposes(y_raw[dd, q, t // 2][:, t % 2, :].bitcast(F32), ps)
+            bank["y", dd, q, t] = ps
+
+        def yex(dd, q, t):
+            tp = t // 2
+            if (dd, q, tp) not in gy:
+                gy[dd, q, tp] = work.tile([P, 2, 2, P, 4], BF16, name="gy", bufs=4, align_bytes=64)
+            dst = gy[dd, q, tp][:, t % 2].rearrange("p g m t -> p (g m t)").bitcast(F32)
+            nc.scalar.copy(
+                out=dst.rearrange("p (g m u) -> p g m u", g=2, u=2),
+                in_=bank["y", dd, q, t][:].rearrange("p g u m -> p g m u"),
+            )
+
+        def yq(dd, q, tp):
+            y_codes[dd, q, tp] = work.tile([P, 2, 2, P], U32, name="y_codes", bufs=8, align_bytes=64)
+            y_scales[dd, q, tp] = work.tile([P, 2, 2, P], U8, name="y_scales", bufs=8, align_bytes=64)
+            nc.vector.quantize_mx(
+                out=y_codes[dd, q, tp][:].rearrange("p b g f -> p (b g f)").bitcast(FP8X4),
+                scales=y_scales[dd, q, tp][:].rearrange("p b g f -> p (b g f)"),
+                in_=gy[dd, q, tp][:].rearrange("p b g f t -> p (b g f t)"),
+            )
+
+        def xint(dd, q, kq):
+            if (dd, q) not in gx:
+                gx[dd, q] = work.tile([P, K, 4], BF16, name="gx", bufs=3, align_bytes=64)
+            ks = slice(128 * kq, 128 * (kq + 1))
+            nc.scalar.copy(out=gx[dd, q][:, ks, :], in_=x_raw[dd, q][:, :, ks].rearrange("p t k -> p k t"))
+
+        def xq(dd, q):
+            x_codes[dd, q] = work.tile([P, K], U32, name="x_codes", bufs=4, align_bytes=64)
+            x_scales[dd, q] = work.tile([P, K], U8, name="x_scales", bufs=4, align_bytes=64)
+            nc.vector.quantize_mx(
+                out=x_codes[dd, q][:].bitcast(FP8X4),
+                scales=x_scales[dd, q][:],
+                in_=gx[dd, q][:].rearrange("p k t -> p (k t)"),
+            )
+
+        def unit(s, i):
+            dd, j = SEQ[s]
+            q, b = divmod(i, 2)
+            ps = psum.tile([P, 4, P], F32, name="unit", bufs=3)
+            for t in range(4):
+                for gi in range(2):
+                    nc.tensor.matmul_mx(
+                        out=ps[:, t, :],
+                        lhsT=y_codes[dd, q, t // 2][:, t % 2, gi, :].bitcast(FP8X4),
+                        lhsT_scale=y_scales[dd, q, t // 2][:, t % 2, gi, :],
+                        rhs=w_codes[j][:, b, gi, :].bitcast(FP8X4),
+                        rhs_scale=w_scales[j][:, b, gi, :],
+                        start=(gi == 0),
+                        stop=(gi == 1),
+                    )
+            bank["u", s, i] = ps
+
+        def dhg(s, i):
+            dd, j = SEQ[s]
+            q, b = divmod(i, 2)
+            if (s, q) not in dh:
+                dh[s, q] = work.tile([P, PF, 4], BF16, name="dh", bufs=4, align_bytes=64)
+            f0 = PF * (j % 2) + P * b
+            nc.vector.tensor_tensor(
+                out=dh[s, q][:, P * b : P * (b + 1), :],
+                in0=bank["u", s, i][:].rearrange("p t f -> p f t"),
+                in1=g_raw[dd, q, j // 2][:, :, f0 : f0 + P].rearrange("p t f -> p f t"),
+                op=MULT,
+            )
+
+        def qd(s, q):
+            d_codes[s, q] = work.tile([P, PF], U32, name="d_codes", bufs=4, align_bytes=64)
+            d_scales[s, q] = work.tile([P, PF], U8, name="d_scales", bufs=4, align_bytes=64)
+            nc.vector.quantize_mx(
+                out=d_codes[s, q][:].bitcast(FP8X4),
+                scales=d_scales[s, q][:],
+                in_=dh[s, q][:].rearrange("p f t -> p (f t)"),
+            )
+
+        def p2(s, h):
+            dd = SEQ[s][0]
+            ps = psum.tile([P, 2, PF], F32, name="p2", bufs=3)
+            for k2 in range(2):
+                kc = slice(P * (2 * h + k2), P * (2 * h + k2 + 1))
+                for q in range(2):
+                    nc.tensor.matmul_mx(
+                        out=ps[:, k2, :],
+                        lhsT=x_codes[dd, q][:, kc].bitcast(FP8X4),
+                        lhsT_scale=x_scales[dd, q][:, kc],
+                        rhs=d_codes[s, q][:].bitcast(FP8X4),
+                        rhs_scale=d_scales[s, q][:],
+                        start=(q == 0),
+                        stop=(q == 1),
+                    )
+            bank["p", s, h] = ps
+
+        def pex(s, h):
+            dd, j = SEQ[s]
+            ps = bank["p", s, h]
+            if dd == 0:
+                acc[j, h] = work.tile([P, 2, PF], F32, name="acc", bufs=12)
+                nc.scalar.activation(out=acc[j, h][:], in_=ps[:], func=COPY, scale=c_all[:, 0:1])
+            else:
+                nc.vector.scalar_tensor_tensor(
+                    out=acc[j, h][:], in0=ps[:], scalar=c_all[:, 1:2], in1=acc[j, h][:], op0=MULT, op1=ADD
+                )
+                nc.sync.dma_start(out=out_view[h][:, :, PF * j : PF * (j + 1)], in_=acc[j, h][:])
+
+        tail = {}
+
+        def tail_pass(q):
+            s = 2 * PAIRS - 1
+            for kt in range(4):
+                if q == 0:
+                    tail[kt] = psum.tile([P, PF], F32, name=("p2", "tr")[kt % 2], bufs=(3, 2)[kt % 2])
+                kc = slice(P * kt, P * (kt + 1))
+                nc.tensor.matmul_mx(
+                    out=tail[kt][:],
+                    lhsT=x_codes[1, q][:, kc].bitcast(FP8X4),
+                    lhsT_scale=x_scales[1, q][:, kc],
+                    rhs=d_codes[s, q][:].bitcast(FP8X4),
+                    rhs_scale=d_scales[s, q][:],
+                    start=(q == 0),
+                    stop=(q == 1),
+                )
+
+        def tail_out():
+            j = PAIRS - 1
+            for kt in range(4):
+                total = acc[j, kt // 2][:, kt % 2, :]
+                nc.vector.scalar_tensor_tensor(
+                    out=total, in0=tail[kt][:], scalar=c_all[:, 1:2], in1=total, op0=MULT, op1=ADD
+                )
+                nc.sync.dma_start(out=out[P * kt : P * (kt + 1), PF * j : PF * (j + 1)], in_=total)
+
+        ytr(0, 0, 0)
+        prod(0)
+        ytr(0, 0, 1)
+        yex(0, 0, 0)
+        yex(0, 0, 1)
+        prod(1)
+        ytr(0, 0, 2)
+        ytr(0, 0, 3)
+        yex(0, 0, 2)
+        yq(0, 0, 0)
+        yex(0, 0, 3)
+        wtr(0)
+        prod(2)
+        wtr(1)
+        wex(0)
+        wex(1)
+        yq(0, 0, 1)
+        ytr(0, 1, 0)
+        ytr(0, 1, 1)
+        wq(0)
+        yex(0, 1, 0)
+        prod(3)
+        yex(0, 1, 1)
+        ytr(0, 1, 2)
+        ytr(0, 1, 3)
+        yex(0, 1, 2)
+        yq(0, 1, 0)
+        unit(0, 0)
+        yex(0, 1, 3)
+        prod(4)
+        unit(0, 1)
+        xint(0, 0, 0)
+        wtr(2)
+        xint(0, 0, 2)
+        yq(0, 1, 1)
+        wtr(3)
+        xint(0, 0, 1)
+        dhg(0, 0)
+        unit(0, 2)
+        dhg(0, 1)
+        wex(2)
+        prod(5)
+        wex(3)
+        unit(0, 3)
+        xint(0, 0, 3)
+        wtr(4)
+        qd(0, 0)
+        xint(0, 1, 1)
+        wq(1)
+        wtr(5)
+        wex(4)
+        dhg(0, 2)
+        unit(1, 0)
+        wex(5)
+        dhg(0, 3)
+        unit(1, 1)
+        xint(0, 1, 3)
+        dhg(1, 0)
+        unit(1, 2)
+        xint(0, 1, 0)
+        qd(0, 1)
+        xq(0, 0)
+        unit(1, 3)
+        xint(0, 1, 2)
+        wq(2)
+        ytr(1, 0, 0)
+        dhg(1, 1)
+        ytr(1, 0, 1)
+        yex(1, 0, 0)
+        xq(0, 1)
+        unit(2, 0)
+        yex(1, 0, 1)
+        qd(1, 0)
+        prod(6)
+        p2(0, 0)
+        p2(0, 1)
+        pex(0, 0)
+        dhg(1, 2)
+        wtr(6)
+        pex(0, 1)
+        prod(7)
+        unit(2, 1)
+        wex(6)
+        ytr(1, 0, 2)
+        dhg(1, 3)
+        wtr(7)
+        dhg(2, 0)
+        yex(1, 0, 2)
+        unit(2, 2)
+        qd(1, 1)
+        wex(7)
+        dhg(2, 1)
+        p2(1, 0)
+        xint(1, 0, 1)
+        wq(3)
+        p2(1, 1)
+        qd(2, 0)
+        pex(1, 0)
+        prod(8)
+        unit(2, 3)
+        pex(1, 1)
+        unit(3, 0)
+        xint(1, 0, 3)
+        dhg(2, 2)
+        wtr(8)
+        xint(1, 0, 0)
+        prod(9)
+        ytr(1, 0, 3)
+        wex(8)
+        unit(3, 1)
+        yex(1, 0, 3)
+        dhg(2, 3)
+        wtr(9)
+        xint(1, 0, 2)
+        dhg(3, 0)
+        qd(2, 1)
+        ytr(1, 1, 0)
+        xint(1, 1, 0)
+        dhg(3, 1)
+        p2(2, 0)
+        wex(9)
+        prod(10)
+        yex(1, 1, 0)
+        p2(2, 1)
+        pex(2, 0)
+        unit(3, 2)
+        qd(3, 0)
+        wq(4)
+        pex(2, 1)
+        unit(3, 3)
+        dhg(3, 2)
+        xint(1, 1, 2)
+        unit(4, 0)
+        prod(11)
+        xint(1, 1, 1)
+        unit(4, 1)
+        xint(1, 1, 3)
+        wtr(10)
+        dhg(3, 3)
+        load_g(1, 0, 1)
+        load_g(1, 1, 1)
+        wtr(11)
+        dhg(4, 0)
+        wex(10)
+        unit(4, 2)
+        qd(3, 1)
+        wex(11)
+        dhg(4, 1)
+        p2(3, 0)
+        wq(5)
+        p2(3, 1)
+        pex(3, 0)
+        qd(4, 0)
+        dhg(4, 2)
+        unit(4, 3)
+        pex(3, 1)
+        yq(1, 0, 0)
+        unit(5, 0)
+        dhg(4, 3)
+        unit(5, 1)
+        dhg(5, 0)
+        unit(5, 2)
+        qd(4, 1)
+        ytr(1, 1, 1)
+        yq(1, 0, 1)
+        dhg(5, 1)
+        ytr(1, 1, 2)
+        yex(1, 1, 1)
+        p2(4, 0)
+        dhg(5, 2)
+        yex(1, 1, 2)
+        qd(5, 0)
+        p2(4, 1)
+        yq(1, 1, 0)
+        pex(4, 0)
+        ytr(1, 1, 3)
+        xq(1, 0)
+        pex(4, 1)
+        unit(5, 3)
+        xq(1, 1)
+        yex(1, 1, 3)
+        unit(6, 0)
+        yq(1, 1, 1)
+        unit(6, 1)
+        dhg(5, 3)
+        load_g(1, 0, 2)
+        load_g(1, 1, 2)
+        dhg(6, 0)
+        unit(6, 2)
+        qd(5, 1)
+        unit(6, 3)
+        dhg(6, 1)
+        p2(5, 0)
+        dhg(6, 2)
+        p2(5, 1)
+        qd(6, 0)
+        pex(5, 0)
+        dhg(6, 3)
+        unit(7, 0)
+        pex(5, 1)
+        qd(6, 1)
+        unit(7, 1)
+        dhg(7, 0)
+        p2(6, 0)
+        dhg(7, 1)
+        p2(6, 1)
+        pex(6, 0)
+        unit(7, 2)
+        qd(7, 0)
+        pex(6, 1)
+        unit(7, 3)
+        dhg(7, 2)
+        unit(8, 0)
+        dhg(7, 3)
+        unit(8, 1)
+        dhg(8, 0)
+        unit(8, 2)
+        qd(7, 1)
+        dhg(8, 1)
+        p2(7, 0)
+        dhg(8, 2)
+        p2(7, 1)
+        qd(8, 0)
+        unit(8, 3)
+        pex(7, 0)
+        unit(9, 0)
+        dhg(8, 3)
+        unit(9, 1)
+        dhg(9, 0)
+        unit(9, 2)
+        qd(8, 1)
+        dhg(9, 1)
+        p2(8, 0)
+        dhg(9, 2)
+        p2(8, 1)
+        qd(9, 0)
+        unit(9, 3)
+        pex(7, 1)
+        unit(10, 0)
+        pex(8, 0)
+        dhg(9, 3)
+        unit(10, 1)
+        dhg(10, 0)
+        unit(10, 2)
+        qd(9, 1)
+        unit(10, 3)
+        dhg(10, 1)
+        p2(9, 0)
+        dhg(10, 2)
+        p2(9, 1)
+        qd(10, 0)
+        dhg(10, 3)
+        unit(11, 0)
+        pex(8, 1)
+        unit(11, 1)
+        qd(10, 1)
+        dhg(11, 0)
+        p2(10, 0)
+        dhg(11, 1)
+        unit(11, 2)
+        pex(9, 0)
+        unit(11, 3)
+        qd(11, 0)
+        tail_pass(0)
+        p2(10, 1)
+        dhg(11, 2)
+        dhg(11, 3)
+        pex(9, 1)
+        qd(11, 1)
+        tail_pass(1)
+        pex(10, 0)
+        pex(10, 1)
+        tail_out()

@@ -20,7 +20,7 @@ P = 128
 HALVES = 2
 PAIRS = 6
 PF = 256
-SEQ = [(0, j) for j in range(6)] + [(1, j) for j in range(6)]
+SEQ = ((0,0),(0,1),(0,2),(0,3),(1,0),(0,4),(1,1),(0,5),(1,2),(1,3),(1,4),(1,5))
 
 
 def tile_shard_weight_grad_s7_kernel(tc, x, dy, w2_bytes, w2_scale, g, c, out):
@@ -62,10 +62,10 @@ def tile_shard_weight_grad_s7_kernel(tc, x, dy, w2_bytes, w2_scale, g, c, out):
                 in_=g[dd].rearrange("(q p t) f -> q p t f", q=2, t=4)[q][:, :, 512 * ch : 512 * (ch + 1)],
             )
 
-        load_w(0)
         load_y(0, 0, 0)
-        load_w(1)
+        load_w(0)
         load_y(0, 0, 1)
+        load_w(1)
         load_y(0, 1, 0)
         load_w(2)
         load_y(0, 1, 1)
@@ -76,20 +76,30 @@ def tile_shard_weight_grad_s7_kernel(tc, x, dy, w2_bytes, w2_scale, g, c, out):
         load_w(3)
         load_g(0, 0, 1)
         load_g(0, 1, 1)
+        load_y(1, 0, 0)
+        load_y(1, 0, 1)
+        load_y(1, 1, 0)
+        load_y(1, 1, 1)
         load_w(4)
-        load_w(5)
-        for q in range(2):
-            for tp in range(2):
-                load_y(1, q, tp)
-        load_g(0, 0, 2)
-        load_g(0, 1, 2)
         load_x(1, 0)
-        load_x(1, 1)
         load_g(1, 0, 0)
+        load_x(1, 1)
         load_g(1, 1, 0)
+        load_g(0, 0, 2)
+        load_w(5)
+        load_g(0, 1, 2)
 
         ident = keep.tile([P, P], F32, name="ident", align_bytes=64)
         make_identity(nc, ident[:])
+        zeros = keep.tile([P, 512], BF16, name="zeros", align_bytes=64)
+        nc.vector.memset(zeros[:], 0.0)
+
+        def warm(n):
+            for i in range(n):
+                ps = psum.tile([P, 512], F32, name="p2", bufs=3)
+                nc.tensor.matmul(ps[:], lhsT=zeros[:, 0:P], rhs=zeros[:], start=True, stop=True)
+
+        warm(4)
         scale_all = keep.tile([P, P, 8], F32, name="scale_all", align_bytes=64)
         for h in range(2):
             ps = psum.tile([P, 4, P], F32, name="tr", bufs=2)
@@ -112,7 +122,7 @@ def tile_shard_weight_grad_s7_kernel(tc, x, dy, w2_bytes, w2_scale, g, c, out):
         acc = {}
 
         def prod(b):
-            wb[b] = work.tile([P, N], BF16, name="wb", bufs=7, align_bytes=64)
+            wb[b] = work.tile([P, N], BF16, name="wb", bufs=8, align_bytes=64)
             nc.vector.tensor_tensor(
                 out=wb[b][:],
                 in0=w_raw[b // 2][:, b % 2, :].bitcast(FP8),
@@ -133,7 +143,7 @@ def tile_shard_weight_grad_s7_kernel(tc, x, dy, w2_bytes, w2_scale, g, c, out):
         def wex(b):
             j = b // 2
             if j not in gw:
-                gw[j] = work.tile([P, 2, 2, P, 4], BF16, name="gw", bufs=2, align_bytes=64)
+                gw[j] = work.tile([P, 2, 2, P, 4], BF16, name="gw", bufs=3, align_bytes=64)
             dst = gw[j][:, b % 2].rearrange("p g f t -> p (g f t)").bitcast(F32)
             nc.scalar.copy(
                 out=dst.rearrange("p (g f u) -> p g f u", g=2, u=2),
@@ -175,7 +185,7 @@ def tile_shard_weight_grad_s7_kernel(tc, x, dy, w2_bytes, w2_scale, g, c, out):
 
         def xint(dd, q, kq):
             if (dd, q) not in gx:
-                gx[dd, q] = work.tile([P, K, 4], BF16, name="gx", bufs=3, align_bytes=64)
+                gx[dd, q] = work.tile([P, K, 4], BF16, name="gx", bufs=2, align_bytes=64)
             ks = slice(128 * kq, 128 * (kq + 1))
             nc.scalar.copy(out=gx[dd, q][:, ks, :], in_=x_raw[dd, q][:, :, ks].rearrange("p t k -> p k t"))
 
@@ -262,7 +272,7 @@ def tile_shard_weight_grad_s7_kernel(tc, x, dy, w2_bytes, w2_scale, g, c, out):
             s = 2 * PAIRS - 1
             for kt in range(4):
                 if q == 0:
-                    tail[kt] = psum.tile([P, PF], F32, name=("p2", "tr")[kt % 2], bufs=(3, 2)[kt % 2])
+                    tail[kt] = psum.tile([P, PF], F32, name=("tr", "unit")[kt // 2], bufs=(2, 3)[kt // 2])
                 kc = slice(P * kt, P * (kt + 1))
                 nc.tensor.matmul_mx(
                     out=tail[kt][:],
@@ -283,276 +293,281 @@ def tile_shard_weight_grad_s7_kernel(tc, x, dy, w2_bytes, w2_scale, g, c, out):
                 )
                 nc.sync.dma_start(out=out[P * kt : P * (kt + 1), PF * j : PF * (j + 1)], in_=total)
 
+        warm(1)
         ytr(0, 0, 0)
-        prod(0)
         ytr(0, 0, 1)
+        prod(0)
         yex(0, 0, 0)
         yex(0, 0, 1)
-        prod(1)
+        warm(1)
         ytr(0, 0, 2)
-        ytr(0, 0, 3)
-        yex(0, 0, 2)
-        yq(0, 0, 0)
-        yex(0, 0, 3)
+        prod(1)
         wtr(0)
+        yex(0, 0, 2)
         prod(2)
-        wtr(1)
+        warm(1)
+        ytr(0, 0, 3)
         wex(0)
-        wex(1)
-        yq(0, 0, 1)
+        prod(3)
+        wtr(1)
+        yex(0, 0, 3)
+        warm(1)
         ytr(0, 1, 0)
+        wex(1)
+        yq(0, 0, 0)
         ytr(0, 1, 1)
         wq(0)
         yex(0, 1, 0)
-        prod(3)
-        yex(0, 1, 1)
+        yq(0, 0, 1)
+        warm(1)
         ytr(0, 1, 2)
+        yex(0, 1, 1)
+        prod(4)
         ytr(0, 1, 3)
         yex(0, 1, 2)
-        yq(0, 1, 0)
         unit(0, 0)
+        yq(0, 1, 0)
         yex(0, 1, 3)
-        prod(4)
-        unit(0, 1)
-        xint(0, 0, 0)
         wtr(2)
-        xint(0, 0, 2)
-        yq(0, 1, 1)
-        wtr(3)
-        xint(0, 0, 1)
-        dhg(0, 0)
-        unit(0, 2)
-        dhg(0, 1)
-        wex(2)
         prod(5)
+        xint(0, 0, 0)
+        wtr(3)
+        xint(0, 0, 2)
+        unit(0, 1)
+        dhg(0, 0)
+        wex(2)
+        yq(0, 1, 1)
         wex(3)
-        unit(0, 3)
-        xint(0, 0, 3)
         wtr(4)
-        qd(0, 0)
-        xint(0, 1, 1)
-        wq(1)
+        dhg(0, 1)
+        xint(0, 0, 1)
         wtr(5)
-        wex(4)
+        wq(1)
+        xint(0, 0, 3)
+        unit(0, 2)
+        qd(0, 0)
+        xint(0, 1, 0)
+        xq(0, 0)
+        unit(0, 3)
+        xint(0, 1, 2)
         dhg(0, 2)
         unit(1, 0)
-        wex(5)
+        xint(0, 1, 1)
         dhg(0, 3)
         unit(1, 1)
         xint(0, 1, 3)
         dhg(1, 0)
         unit(1, 2)
-        xint(0, 1, 0)
-        qd(0, 1)
-        xq(0, 0)
-        unit(1, 3)
-        xint(0, 1, 2)
-        wq(2)
-        ytr(1, 0, 0)
+        wex(4)
         dhg(1, 1)
-        ytr(1, 0, 1)
-        yex(1, 0, 0)
+        load_g(1, 0, 1)
+        unit(1, 3)
+        wex(5)
         xq(0, 1)
-        unit(2, 0)
-        yex(1, 0, 1)
-        qd(1, 0)
-        prod(6)
-        p2(0, 0)
-        p2(0, 1)
-        pex(0, 0)
+        ytr(1, 0, 0)
         dhg(1, 2)
-        wtr(6)
-        pex(0, 1)
-        prod(7)
-        unit(2, 1)
-        wex(6)
-        ytr(1, 0, 2)
+        ytr(1, 0, 1)
+        qd(0, 1)
+        yex(1, 0, 0)
         dhg(1, 3)
-        wtr(7)
+        load_g(1, 1, 1)
+        p2(0, 0)
+        yex(1, 0, 1)
+        wq(2)
+        p2(0, 1)
+        qd(1, 0)
+        pex(0, 0)
+        unit(2, 0)
+        prod(6)
+        pex(0, 1)
+        unit(2, 1)
         dhg(2, 0)
-        yex(1, 0, 2)
-        unit(2, 2)
-        qd(1, 1)
-        wex(7)
+        wtr(6)
         dhg(2, 1)
-        p2(1, 0)
-        xint(1, 0, 1)
-        wq(3)
-        p2(1, 1)
-        qd(2, 0)
-        pex(1, 0)
-        prod(8)
+        ytr(1, 0, 2)
+        prod(7)
+        wex(6)
+        unit(2, 2)
+        yex(1, 0, 2)
         unit(2, 3)
-        pex(1, 1)
-        unit(3, 0)
-        xint(1, 0, 3)
+        qd(1, 1)
+        xint(1, 0, 1)
         dhg(2, 2)
-        wtr(8)
-        xint(1, 0, 0)
-        prod(9)
-        ytr(1, 0, 3)
-        wex(8)
-        unit(3, 1)
-        yex(1, 0, 3)
+        p2(1, 0)
+        xint(1, 0, 3)
         dhg(2, 3)
-        wtr(9)
-        xint(1, 0, 2)
-        dhg(3, 0)
+        p2(1, 1)
+        pex(1, 0)
+        qd(2, 0)
+        wtr(7)
         qd(2, 1)
-        ytr(1, 1, 0)
-        xint(1, 1, 0)
-        dhg(3, 1)
+        pex(1, 1)
+        prod(8)
+        ytr(1, 0, 3)
+        wex(7)
         p2(2, 0)
-        wex(9)
-        prod(10)
-        yex(1, 1, 0)
+        yex(1, 0, 3)
+        prod(9)
         p2(2, 1)
         pex(2, 0)
-        unit(3, 2)
-        qd(3, 0)
-        wq(4)
+        ytr(1, 1, 0)
+        wq(3)
         pex(2, 1)
-        unit(3, 3)
-        dhg(3, 2)
-        xint(1, 1, 2)
-        unit(4, 0)
-        prod(11)
+        ytr(1, 1, 1)
+        yq(1, 0, 0)
+        yex(1, 1, 0)
+        unit(3, 0)
+        yq(1, 0, 1)
+        yex(1, 1, 1)
+        unit(3, 1)
+        prod(10)
+        xint(1, 0, 0)
+        unit(3, 2)
+        xint(1, 0, 2)
+        dhg(3, 0)
+        ytr(1, 1, 2)
         xint(1, 1, 1)
-        unit(4, 1)
+        dhg(3, 1)
+        load_g(1, 0, 2)
+        ytr(1, 1, 3)
         xint(1, 1, 3)
-        wtr(10)
+        dhg(3, 2)
+        unit(3, 3)
+        yex(1, 1, 2)
+        qd(3, 0)
+        yex(1, 1, 3)
+        yq(1, 1, 0)
+        unit(4, 0)
+        xint(1, 1, 0)
         dhg(3, 3)
-        load_g(1, 0, 1)
-        load_g(1, 1, 1)
-        wtr(11)
+        load_g(1, 1, 2)
+        wtr(8)
+        xint(1, 1, 2)
         dhg(4, 0)
-        wex(10)
-        unit(4, 2)
+        wtr(9)
+        wex(8)
         qd(3, 1)
-        wex(11)
-        dhg(4, 1)
+        unit(4, 1)
+        yq(1, 1, 1)
+        wex(9)
         p2(3, 0)
-        wq(5)
+        xq(1, 0)
         p2(3, 1)
+        dhg(4, 1)
         pex(3, 0)
+        unit(4, 2)
+        wq(4)
+        pex(3, 1)
+        unit(4, 3)
         qd(4, 0)
         dhg(4, 2)
-        unit(4, 3)
-        pex(3, 1)
-        yq(1, 0, 0)
         unit(5, 0)
         dhg(4, 3)
         unit(5, 1)
         dhg(5, 0)
         unit(5, 2)
-        qd(4, 1)
-        ytr(1, 1, 1)
-        yq(1, 0, 1)
         dhg(5, 1)
-        ytr(1, 1, 2)
-        yex(1, 1, 1)
-        p2(4, 0)
-        dhg(5, 2)
-        yex(1, 1, 2)
-        qd(5, 0)
-        p2(4, 1)
-        yq(1, 1, 0)
-        pex(4, 0)
-        ytr(1, 1, 3)
-        xq(1, 0)
-        pex(4, 1)
         unit(5, 3)
         xq(1, 1)
-        yex(1, 1, 3)
         unit(6, 0)
-        yq(1, 1, 1)
-        unit(6, 1)
+        dhg(5, 2)
+        wtr(10)
+        qd(4, 1)
         dhg(5, 3)
-        load_g(1, 0, 2)
-        load_g(1, 1, 2)
+        p2(4, 0)
+        wex(10)
         dhg(6, 0)
+        p2(4, 1)
+        qd(5, 0)
+        unit(6, 1)
+        prod(11)
         unit(6, 2)
-        qd(5, 1)
-        unit(6, 3)
         dhg(6, 1)
-        p2(5, 0)
+        wtr(11)
         dhg(6, 2)
-        p2(5, 1)
-        qd(6, 0)
-        pex(5, 0)
+        unit(6, 3)
+        qd(5, 1)
+        wex(11)
+        pex(4, 0)
+        p2(5, 0)
         dhg(6, 3)
-        unit(7, 0)
+        p2(5, 1)
+        pex(5, 0)
+        wq(5)
+        unit(8, 0)
         pex(5, 1)
-        qd(6, 1)
+        qd(6, 0)
+        unit(7, 0)
+        pex(4, 1)
         unit(7, 1)
+        qd(6, 1)
         dhg(7, 0)
         p2(6, 0)
         dhg(7, 1)
         p2(6, 1)
-        pex(6, 0)
+        dhg(8, 0)
         unit(7, 2)
         qd(7, 0)
-        pex(6, 1)
         unit(7, 3)
+        pex(6, 0)
         dhg(7, 2)
-        unit(8, 0)
-        dhg(7, 3)
         unit(8, 1)
-        dhg(8, 0)
+        dhg(7, 3)
         unit(8, 2)
-        qd(7, 1)
         dhg(8, 1)
-        p2(7, 0)
-        dhg(8, 2)
-        p2(7, 1)
-        qd(8, 0)
         unit(8, 3)
-        pex(7, 0)
+        dhg(8, 2)
         unit(9, 0)
+        qd(7, 1)
         dhg(8, 3)
         unit(9, 1)
         dhg(9, 0)
+        p2(7, 0)
+        qd(8, 0)
+        p2(7, 1)
+        pex(6, 1)
+        pex(7, 0)
         unit(9, 2)
-        qd(8, 1)
         dhg(9, 1)
-        p2(8, 0)
+        pex(7, 1)
+        unit(9, 3)
         dhg(9, 2)
+        unit(10, 0)
+        qd(8, 1)
+        dhg(9, 3)
+        p2(8, 0)
+        dhg(10, 0)
         p2(8, 1)
         qd(9, 0)
-        unit(9, 3)
-        pex(7, 1)
-        unit(10, 0)
-        pex(8, 0)
-        dhg(9, 3)
         unit(10, 1)
-        dhg(10, 0)
-        unit(10, 2)
         qd(9, 1)
-        unit(10, 3)
-        dhg(10, 1)
+        pex(8, 0)
         p2(9, 0)
-        dhg(10, 2)
+        dhg(10, 1)
         p2(9, 1)
-        qd(10, 0)
-        dhg(10, 3)
-        unit(11, 0)
         pex(8, 1)
-        unit(11, 1)
-        qd(10, 1)
-        dhg(11, 0)
-        p2(10, 0)
-        dhg(11, 1)
-        unit(11, 2)
+        unit(10, 2)
+        qd(10, 0)
+        unit(10, 3)
         pex(9, 0)
+        dhg(10, 2)
+        unit(11, 0)
+        dhg(10, 3)
+        unit(11, 1)
+        dhg(11, 0)
+        unit(11, 2)
+        dhg(11, 1)
         unit(11, 3)
+        dhg(11, 2)
+        qd(10, 1)
+        dhg(11, 3)
+        p2(10, 0)
         qd(11, 0)
         tail_pass(0)
         p2(10, 1)
-        dhg(11, 2)
-        dhg(11, 3)
         pex(9, 1)
+        pex(10, 0)
         qd(11, 1)
         tail_pass(1)
-        pex(10, 0)
         pex(10, 1)
         tail_out()

@@ -20,6 +20,7 @@ P = 128
 HALVES = 2
 PAIRS = 6
 PF = 256
+RUN = 4
 SEQ = ((0,0),(0,1),(0,2),(0,3),(1,0),(0,4),(1,1),(0,5),(1,2),(1,3),(1,4),(1,5))
 
 
@@ -187,7 +188,10 @@ def tile_shard_weight_grad_s7_kernel(tc, x, dy, w2_bytes, w2_scale, g, c, out):
             if (dd, q) not in gx:
                 gx[dd, q] = work.tile([P, K, 4], BF16, name="gx", bufs=2, align_bytes=64)
             ks = slice(128 * kq, 128 * (kq + 1))
-            nc.scalar.copy(out=gx[dd, q][:, ks, :], in_=x_raw[dd, q][:, :, ks].rearrange("p t k -> p k t"))
+            nc.scalar.copy(
+                out=gx[dd, q][:, ks, :].rearrange("p (c i) t -> p c t i", i=RUN),
+                in_=x_raw[dd, q][:, :, ks].rearrange("p t (c i) -> p c t i", i=RUN),
+            )
 
         def xq(dd, q):
             x_codes[dd, q] = work.tile([P, K], U32, name="x_codes", bufs=4, align_bytes=64)
@@ -222,9 +226,9 @@ def tile_shard_weight_grad_s7_kernel(tc, x, dy, w2_bytes, w2_scale, g, c, out):
                 dh[s, q] = work.tile([P, PF, 4], BF16, name="dh", bufs=4, align_bytes=64)
             f0 = PF * (j % 2) + P * b
             nc.vector.tensor_tensor(
-                out=dh[s, q][:, P * b : P * (b + 1), :],
-                in0=bank["u", s, i][:].rearrange("p t f -> p f t"),
-                in1=g_raw[dd, q, j // 2][:, :, f0 : f0 + P].rearrange("p t f -> p f t"),
+                out=dh[s, q][:, P * b : P * (b + 1), :].rearrange("p (c i) t -> p c t i", i=RUN),
+                in0=bank["u", s, i][:].rearrange("p t (c i) -> p c t i", i=RUN),
+                in1=g_raw[dd, q, j // 2][:, :, f0 : f0 + P].rearrange("p t (c i) -> p c t i", i=RUN),
                 op=MULT,
             )
 

from contextlib import ExitStack

import concourse.mybir as mybir
from concourse.masks import make_identity

D, T, K, N, F = 2, 1024, 512, 1024, 1536
FLOPS = 2 * D * T * N * F + 2 * D * T * K * F

F32 = mybir.dt.float32
BF16 = mybir.dt.bfloat16
U32 = mybir.dt.uint32
U8 = mybir.dt.uint8
FP8 = mybir.dt.float8_e4m3fn
FP8X4 = mybir.dt.float8_e4m3fn_x4
MULT = mybir.AluOpType.mult
ADD = mybir.AluOpType.add
COPY = mybir.ActivationFunctionType.Copy

P = 128
HALVES = 2
PAIRS = 6
PF = 256
RUN = 4
SEQ = ((0,0),(0,1),(0,2),(0,3),(1,0),(0,4),(1,1),(0,5),(1,2),(1,3),(1,4),(1,5))


def tile_shard_weight_grad_s7_kernel(tc, x, dy, w2_bytes, w2_scale, g, c, out):
    nc = tc.nc
    with ExitStack() as ctx:
        keep = ctx.enter_context(tc.tile_pool(name="keep", bufs=1))
        work = ctx.enter_context(tc.tile_pool(name="work", bufs=2))
        psum = ctx.enter_context(tc.psum_pool(name="psum", bufs=2))
        ctx.enter_context(tc.manual_schedule())

        scale_col = keep.tile([P, 8], F32, name="scale_col")
        nc.scalar.dma_start(out=scale_col[:], in_=w2_scale.rearrange("o (p c) -> p (o c)", c=8))
        c_bf = keep.tile([P, D], BF16, name="c_bf")
        nc.scalar.dma_start(out=c_bf[:], in_=c.partition_broadcast(P))

        w_raw, y_raw, x_raw, g_raw = {}, {}, {}, {}
        w_view = w2_bytes.rearrange("(j b p) n -> j p b n", b=2, p=P)
        out_view = out.rearrange("(h kt p) f -> h p kt f", kt=2, p=P)

        def load_w(j):
            w_raw[j] = work.tile([P, 2, N], U8, name="w_raw", bufs=PAIRS)
            nc.sync.dma_start(out=w_raw[j][:], in_=w_view[j])

        def load_y(dd, q, tp):
            y_raw[dd, q, tp] = work.tile([P, 2, N], BF16, name="y_raw", bufs=8, align_bytes=64)
            nc.sync.dma_start(
                out=y_raw[dd, q, tp][:],
                in_=dy[dd].rearrange("(q p t) n -> q p t n", q=2, t=4)[q][:, 2 * tp : 2 * tp + 2, :],
            )

        def load_x(dd, q):
            x_raw[dd, q] = work.tile([P, 4, K], BF16, name="x_raw", bufs=4, align_bytes=64)
            nc.sync.dma_start(out=x_raw[dd, q][:], in_=x[dd].rearrange("(q p t) k -> q p t k", q=2, t=4)[q])

        def load_g(dd, q, ch):
            g_raw[dd, q, ch] = work.tile([P, 4, 512], BF16, name="g_raw", bufs=8, align_bytes=64)
            nc.sync.dma_start(
                out=g_raw[dd, q, ch][:],
                in_=g[dd].rearrange("(q p t) f -> q p t f", q=2, t=4)[q][:, :, 512 * ch : 512 * (ch + 1)],
            )

        load_y(0, 0, 0)
        load_w(0)
        load_y(0, 0, 1)
        load_w(1)
        load_y(0, 1, 0)
        load_w(2)
        load_y(0, 1, 1)
        load_g(0, 0, 0)
        load_x(0, 0)
        load_g(0, 1, 0)
        load_x(0, 1)
        load_w(3)
        load_g(0, 0, 1)
        load_g(0, 1, 1)
        load_y(1, 0, 0)
        load_y(1, 0, 1)
        load_y(1, 1, 0)
        load_y(1, 1, 1)
        load_w(4)
        load_x(1, 0)
        load_g(1, 0, 0)
        load_x(1, 1)
        load_g(1, 1, 0)
        load_g(0, 0, 2)
        load_w(5)
        load_g(0, 1, 2)

        ident = keep.tile([P, P], F32, name="ident", align_bytes=64)
        make_identity(nc, ident[:])
        zeros = keep.tile([P, 512], BF16, name="zeros", align_bytes=64)
        nc.vector.memset(zeros[:], 0.0)

        def warm(n):
            for i in range(n):
                ps = psum.tile([P, 512], F32, name="p2", bufs=3)
                nc.tensor.matmul(ps[:], lhsT=zeros[:, 0:P], rhs=zeros[:], start=True, stop=True)

        warm(4)
        scale_all = keep.tile([P, P, 8], F32, name="scale_all", align_bytes=64)
        for h in range(2):
            ps = psum.tile([P, 4, P], F32, name="tr", bufs=2)
            for cc in range(4):
                col = 4 * h + cc
                nc.tensor.transpose(ps[:, cc, :], scale_col[:, col : col + 1].to_broadcast([P, P]), ident[:])
            view = ps[:].rearrange("p c j -> p j c")
            if h == 0:
                nc.scalar.copy(out=scale_all[:, :, 0:4], in_=view)
            else:
                nc.vector.tensor_copy(out=scale_all[:, :, 4:8], in_=view)
        c_all = keep.tile([P, D], F32, name="c_all")
        nc.scalar.copy(out=c_all[:], in_=c_bf[:])

        wb, gw, w_codes, w_scales = {}, {}, {}, {}
        gy, y_codes, y_scales = {}, {}, {}
        x_codes, x_scales, gx = {}, {}, {}
        bank = {}
        dh, d_codes, d_scales = {}, {}, {}
        acc = {}

        def prod(b):
            wb[b] = work.tile([P, N], BF16, name="wb", bufs=8, align_bytes=64)
            nc.vector.tensor_tensor(
                out=wb[b][:],
                in0=w_raw[b // 2][:, b % 2, :].bitcast(FP8),
                in1=scale_all[:].rearrange("p j c -> p (j c)"),
                op=MULT,
            )

        def word_transposes(words, ps):
            for gi in range(2):
                for u in range(2):
                    nc.tensor.transpose(ps[:, gi, u, :], words[:, 256 * gi + u : 256 * (gi + 1) : 2], ident[:])

        def wtr(b):
            ps = psum.tile([P, 2, 2, P], F32, name="tr", bufs=2)
            word_transposes(wb[b][:].bitcast(F32), ps)
            bank["w", b] = ps

        def wex(b):
            j = b // 2
            if j not in gw:
                gw[j] = work.tile([P, 2, 2, P, 4], BF16, name="gw", bufs=3, align_bytes=64)
            dst = gw[j][:, b % 2].rearrange("p g f t -> p (g f t)").bitcast(F32)
            nc.scalar.copy(
                out=dst.rearrange("p (g f u) -> p g f u", g=2, u=2),
                in_=bank["w", b][:].rearrange("p g u f -> p g f u"),
            )

        def wq(j):
            w_codes[j] = work.tile([P, 2, 2, P], U32, name="w_codes", bufs=PAIRS, align_bytes=64)
            w_scales[j] = work.tile([P, 2, 2, P], U8, name="w_scales", bufs=PAIRS, align_bytes=64)
            nc.vector.quantize_mx(
                out=w_codes[j][:].rearrange("p b g f -> p (b g f)").bitcast(FP8X4),
                scales=w_scales[j][:].rearrange("p b g f -> p (b g f)"),
                in_=gw[j][:].rearrange("p b g f t -> p (b g f t)"),
            )

        def ytr(dd, q, t):
            ps = psum.tile([P, 2, 2, P], F32, name="tr", bufs=2)
            word_transposes(y_raw[dd, q, t // 2][:, t % 2, :].bitcast(F32), ps)
            bank["y", dd, q, t] = ps

        def yex(dd, q, t):
            tp = t // 2
            if (dd, q, tp) not in gy:
                gy[dd, q, tp] = work.tile([P, 2, 2, P, 4], BF16, name="gy", bufs=4, align_bytes=64)
            dst = gy[dd, q, tp][:, t % 2].rearrange("p g m t -> p (g m t)").bitcast(F32)
            nc.scalar.copy(
                out=dst.rearrange("p (g m u) -> p g m u", g=2, u=2),
                in_=bank["y", dd, q, t][:].rearrange("p g u m -> p g m u"),
            )

        def yq(dd, q, tp):
            y_codes[dd, q, tp] = work.tile([P, 2, 2, P], U32, name="y_codes", bufs=8, align_bytes=64)
            y_scales[dd, q, tp] = work.tile([P, 2, 2, P], U8, name="y_scales", bufs=8, align_bytes=64)
            nc.vector.quantize_mx(
                out=y_codes[dd, q, tp][:].rearrange("p b g f -> p (b g f)").bitcast(FP8X4),
                scales=y_scales[dd, q, tp][:].rearrange("p b g f -> p (b g f)"),
                in_=gy[dd, q, tp][:].rearrange("p b g f t -> p (b g f t)"),
            )

        def xint(dd, q, kq):
            if (dd, q) not in gx:
                gx[dd, q] = work.tile([P, K, 4], BF16, name="gx", bufs=2, align_bytes=64)
            ks = slice(128 * kq, 128 * (kq + 1))
            nc.scalar.copy(
                out=gx[dd, q][:, ks, :].rearrange("p (c i) t -> p c t i", i=RUN),
                in_=x_raw[dd, q][:, :, ks].rearrange("p t (c i) -> p c t i", i=RUN),
            )

        def xq(dd, q):
            x_codes[dd, q] = work.tile([P, K], U32, name="x_codes", bufs=4, align_bytes=64)
            x_scales[dd, q] = work.tile([P, K], U8, name="x_scales", bufs=4, align_bytes=64)
            nc.vector.quantize_mx(
                out=x_codes[dd, q][:].bitcast(FP8X4),
                scales=x_scales[dd, q][:],
                in_=gx[dd, q][:].rearrange("p k t -> p (k t)"),
            )

        def unit(s, i):
            dd, j = SEQ[s]
            q, b = divmod(i, 2)
            ps = psum.tile([P, 4, P], F32, name="unit", bufs=3)
            for t in range(4):
                for gi in range(2):
                    nc.tensor.matmul_mx(
                        out=ps[:, t, :],
                        lhsT=y_codes[dd, q, t // 2][:, t % 2, gi, :].bitcast(FP8X4),
                        lhsT_scale=y_scales[dd, q, t // 2][:, t % 2, gi, :],
                        rhs=w_codes[j][:, b, gi, :].bitcast(FP8X4),
                        rhs_scale=w_scales[j][:, b, gi, :],
                        start=(gi == 0),
                        stop=(gi == 1),
                    )
            bank["u", s, i] = ps

        def dhg(s, i):
            dd, j = SEQ[s]
            q, b = divmod(i, 2)
            if (s, q) not in dh:
                dh[s, q] = work.tile([P, PF, 4], BF16, name="dh", bufs=4, align_bytes=64)
            f0 = PF * (j % 2) + P * b
            nc.vector.tensor_tensor(
                out=dh[s, q][:, P * b : P * (b + 1), :].rearrange("p (c i) t -> p c t i", i=RUN),
                in0=bank["u", s, i][:].rearrange("p t (c i) -> p c t i", i=RUN),
                in1=g_raw[dd, q, j // 2][:, :, f0 : f0 + P].rearrange("p t (c i) -> p c t i", i=RUN),
                op=MULT,
            )

        def qd(s, q):
            d_codes[s, q] = work.tile([P, PF], U32, name="d_codes", bufs=4, align_bytes=64)
            d_scales[s, q] = work.tile([P, PF], U8, name="d_scales", bufs=4, align_bytes=64)
            nc.vector.quantize_mx(
                out=d_codes[s, q][:].bitcast(FP8X4),
                scales=d_scales[s, q][:],
                in_=dh[s, q][:].rearrange("p f t -> p (f t)"),
            )

        def p2(s, h):
            dd = SEQ[s][0]
            ps = psum.tile([P, 2, PF], F32, name="p2", bufs=3)
            for k2 in range(2):
                kc = slice(P * (2 * h + k2), P * (2 * h + k2 + 1))
                for q in range(2):
                    nc.tensor.matmul_mx(
                        out=ps[:, k2, :],
                        lhsT=x_codes[dd, q][:, kc].bitcast(FP8X4),
                        lhsT_scale=x_scales[dd, q][:, kc],
                        rhs=d_codes[s, q][:].bitcast(FP8X4),
                        rhs_scale=d_scales[s, q][:],
                        start=(q == 0),
                        stop=(q == 1),
                    )
            bank["p", s, h] = ps

        def pex(s, h):
            dd, j = SEQ[s]
            ps = bank["p", s, h]
            if dd == 0:
                acc[j, h] = work.tile([P, 2, PF], F32, name="acc", bufs=12)
                nc.scalar.activation(out=acc[j, h][:], in_=ps[:], func=COPY, scale=c_all[:, 0:1])
            else:
                nc.vector.scalar_tensor_tensor(
                    out=acc[j, h][:], in0=ps[:], scalar=c_all[:, 1:2], in1=acc[j, h][:], op0=MULT, op1=ADD
                )
                nc.sync.dma_start(out=out_view[h][:, :, PF * j : PF * (j + 1)], in_=acc[j, h][:])

        tail = {}

        def tail_pass(q):
            s = 2 * PAIRS - 1
            for kt in range(4):
                if q == 0:
                    tail[kt] = psum.tile([P, PF], F32, name=("tr", "unit")[kt // 2], bufs=(2, 3)[kt // 2])
                kc = slice(P * kt, P * (kt + 1))
                nc.tensor.matmul_mx(
                    out=tail[kt][:],
                    lhsT=x_codes[1, q][:, kc].bitcast(FP8X4),
                    lhsT_scale=x_scales[1, q][:, kc],
                    rhs=d_codes[s, q][:].bitcast(FP8X4),
                    rhs_scale=d_scales[s, q][:],
                    start=(q == 0),
                    stop=(q == 1),
                )

        def tail_out():
            j = PAIRS - 1
            for kt in range(4):
                total = acc[j, kt // 2][:, kt % 2, :]
                nc.vector.scalar_tensor_tensor(
                    out=total, in0=tail[kt][:], scalar=c_all[:, 1:2], in1=total, op0=MULT, op1=ADD
                )
                nc.sync.dma_start(out=out[P * kt : P * (kt + 1), PF * j : PF * (j + 1)], in_=total)

        warm(1)
        ytr(0, 0, 0)
        ytr(0, 0, 1)
        prod(0)
        yex(0, 0, 0)
        yex(0, 0, 1)
        warm(1)
        ytr(0, 0, 2)
        prod(1)
        wtr(0)
        yex(0, 0, 2)
        prod(2)
        warm(1)
        ytr(0, 0, 3)
        wex(0)
        prod(3)
        wtr(1)
        yex(0, 0, 3)
        warm(1)
        ytr(0, 1, 0)
        wex(1)
        yq(0, 0, 0)
        ytr(0, 1, 1)
        wq(0)
        yex(0, 1, 0)
        yq(0, 0, 1)
        warm(1)
        ytr(0, 1, 2)
        yex(0, 1, 1)
        prod(4)
        ytr(0, 1, 3)
        yex(0, 1, 2)
        unit(0, 0)
        yq(0, 1, 0)
        yex(0, 1, 3)
        wtr(2)
        prod(5)
        xint(0, 0, 0)
        wtr(3)
        xint(0, 0, 2)
        unit(0, 1)
        dhg(0, 0)
        wex(2)
        yq(0, 1, 1)
        wex(3)
        wtr(4)
        dhg(0, 1)
        xint(0, 0, 1)
        wtr(5)
        wq(1)
        xint(0, 0, 3)
        unit(0, 2)
        qd(0, 0)
        xint(0, 1, 0)
        xq(0, 0)
        unit(0, 3)
        xint(0, 1, 2)
        dhg(0, 2)
        unit(1, 0)
        xint(0, 1, 1)
        dhg(0, 3)
        unit(1, 1)
        xint(0, 1, 3)
        dhg(1, 0)
        unit(1, 2)
        wex(4)
        dhg(1, 1)
        load_g(1, 0, 1)
        unit(1, 3)
        wex(5)
        xq(0, 1)
        ytr(1, 0, 0)
        dhg(1, 2)
        ytr(1, 0, 1)
        qd(0, 1)
        yex(1, 0, 0)
        dhg(1, 3)
        load_g(1, 1, 1)
        p2(0, 0)
        yex(1, 0, 1)
        wq(2)
        p2(0, 1)
        qd(1, 0)
        pex(0, 0)
        unit(2, 0)
        prod(6)
        pex(0, 1)
        unit(2, 1)
        dhg(2, 0)
        wtr(6)
        dhg(2, 1)
        ytr(1, 0, 2)
        prod(7)
        wex(6)
        unit(2, 2)
        yex(1, 0, 2)
        unit(2, 3)
        qd(1, 1)
        xint(1, 0, 1)
        dhg(2, 2)
        p2(1, 0)
        xint(1, 0, 3)
        dhg(2, 3)
        p2(1, 1)
        pex(1, 0)
        qd(2, 0)
        wtr(7)
        qd(2, 1)
        pex(1, 1)
        prod(8)
        ytr(1, 0, 3)
        wex(7)
        p2(2, 0)
        yex(1, 0, 3)
        prod(9)
        p2(2, 1)
        pex(2, 0)
        ytr(1, 1, 0)
        wq(3)
        pex(2, 1)
        ytr(1, 1, 1)
        yq(1, 0, 0)
        yex(1, 1, 0)
        unit(3, 0)
        yq(1, 0, 1)
        yex(1, 1, 1)
        unit(3, 1)
        prod(10)
        xint(1, 0, 0)
        unit(3, 2)
        xint(1, 0, 2)
        dhg(3, 0)
        ytr(1, 1, 2)
        xint(1, 1, 1)
        dhg(3, 1)
        load_g(1, 0, 2)
        ytr(1, 1, 3)
        xint(1, 1, 3)
        dhg(3, 2)
        unit(3, 3)
        yex(1, 1, 2)
        qd(3, 0)
        yex(1, 1, 3)
        yq(1, 1, 0)
        unit(4, 0)
        xint(1, 1, 0)
        dhg(3, 3)
        load_g(1, 1, 2)
        wtr(8)
        xint(1, 1, 2)
        dhg(4, 0)
        wtr(9)
        wex(8)
        qd(3, 1)
        unit(4, 1)
        yq(1, 1, 1)
        wex(9)
        p2(3, 0)
        xq(1, 0)
        p2(3, 1)
        dhg(4, 1)
        pex(3, 0)
        unit(4, 2)
        wq(4)
        pex(3, 1)
        unit(4, 3)
        qd(4, 0)
        dhg(4, 2)
        unit(5, 0)
        dhg(4, 3)
        unit(5, 1)
        dhg(5, 0)
        unit(5, 2)
        dhg(5, 1)
        unit(5, 3)
        xq(1, 1)
        unit(6, 0)
        dhg(5, 2)
        wtr(10)
        qd(4, 1)
        dhg(5, 3)
        p2(4, 0)
        wex(10)
        dhg(6, 0)
        p2(4, 1)
        qd(5, 0)
        unit(6, 1)
        prod(11)
        unit(6, 2)
        dhg(6, 1)
        wtr(11)
        dhg(6, 2)
        unit(6, 3)
        qd(5, 1)
        wex(11)
        pex(4, 0)
        p2(5, 0)
        dhg(6, 3)
        p2(5, 1)
        pex(5, 0)
        wq(5)
        unit(8, 0)
        pex(5, 1)
        qd(6, 0)
        unit(7, 0)
        pex(4, 1)
        unit(7, 1)
        qd(6, 1)
        dhg(7, 0)
        p2(6, 0)
        dhg(7, 1)
        p2(6, 1)
        dhg(8, 0)
        unit(7, 2)
        qd(7, 0)
        unit(7, 3)
        pex(6, 0)
        dhg(7, 2)
        unit(8, 1)
        dhg(7, 3)
        unit(8, 2)
        dhg(8, 1)
        unit(8, 3)
        dhg(8, 2)
        unit(9, 0)
        qd(7, 1)
        dhg(8, 3)
        unit(9, 1)
        dhg(9, 0)
        p2(7, 0)
        qd(8, 0)
        p2(7, 1)
        pex(6, 1)
        pex(7, 0)
        unit(9, 2)
        dhg(9, 1)
        pex(7, 1)
        unit(9, 3)
        dhg(9, 2)
        unit(10, 0)
        qd(8, 1)
        dhg(9, 3)
        p2(8, 0)
        dhg(10, 0)
        p2(8, 1)
        qd(9, 0)
        unit(10, 1)
        qd(9, 1)
        pex(8, 0)
        p2(9, 0)
        dhg(10, 1)
        p2(9, 1)
        pex(8, 1)
        unit(10, 2)
        qd(10, 0)
        unit(10, 3)
        pex(9, 0)
        dhg(10, 2)
        unit(11, 0)
        dhg(10, 3)
        unit(11, 1)
        dhg(11, 0)
        unit(11, 2)
        dhg(11, 1)
        unit(11, 3)
        dhg(11, 2)
        qd(10, 1)
        dhg(11, 3)
        p2(10, 0)
        qd(11, 0)
        tail_pass(0)
        p2(10, 1)
        pex(9, 1)
        pex(10, 0)
        qd(11, 1)
        tail_pass(1)
        pex(10, 1)
        tail_out()
